import numpy as np, ml_dtypes
CORES = [10,34,74,98]
N = 4
BF = ml_dtypes.bfloat16
def gentries(a):
    return np.ascontiguousarray(a.reshape(8, 16, -1).transpose(0, 2, 1)).reshape(8, -1)
def gtable(e):
    e = np.asarray(e); return np.ascontiguousarray(e.reshape(8, -1, 16).transpose(0, 2, 1)).reshape(128, -1).astype(np.int32)
W, TB, K, DE = 4096, 256, 4, 2
def parts(rng):
    b = rng.integers(0, 128, (N, 8, 1, W)) + rng.integers(0, 129, (N, 8, 16, W))
    return np.minimum(b, 255), rng.integers(0, W, (N, 8, TB, 16)), rng.integers(0, N, (8, TB))
def pack(b, h, first):
    return {"bk": np.ascontiguousarray(b.reshape(N, 128, W)).astype(np.float32).astype(BF), "hand": np.stack([gtable(a.reshape(8, -1)) for a in h]),
            "ld": np.ascontiguousarray(np.tile(first[None], (N, 1, 1))).astype(np.int32)}
def setup_inputs(rng):
    b, h, first = parts(rng)
    return pack(b, h, first)
def setup_inputs_suits(rng):
    b, h, first = parts(rng); q = rng.integers(0, 4, (1, 8, TB, 1)); s = np.arange(N)[:, None, None, None]
    m = rng.integers(0, 4, (1, 8, TB, 1)); m[0, :, :4, 0] = np.arange(4)
    one = np.arange(16) == rng.integers(0, 16, (N, 8, TB, 1))
    su = np.where(m == 0, q, np.where(m == 1, (q + s) & 3, np.where(m == 2, np.where(one, q, (q + 1 + (h >> 2) % 3) & 3), h & 3)))
    return pack(b, (h >> 2) * 4 + su, first)
def setup_inputs_ties(rng):
    b, h, first = parts(rng); base = rng.integers(1, 255, (1, 8, 16, 1)); rot = rng.integers(0, 16, (N, 8, 1, W))
    m = rng.choice(np.array([0, 7, 8, 9, 9, 10, 16]), (N, 8, 1, W)); less = rng.integers(0, 2, (N, 8, 1, W))
    v = base + np.where(((np.arange(16)[:, None] + rot) & 15) < m, 1, -less)
    return pack(np.where(rng.random((N, 8, 1, W)) < 0.5, base, v), h, first)
def setup_inputs_alike(rng):
    b, h, first = parts(rng)
    h[:, 0] = (W - 1) * rng.integers(0, 2, (N, TB, 16)); h[:, 1] = h[:1, 1]; h[:, 2] = h[:, 2, :, :1]; h[:, 3] = h[:, 3, :1]
    h[:, 4] = rng.integers(0, 32, (N, TB, 16)); h[:, 5] = W - 1 - rng.integers(0, 16, (N, TB, 16))
    first[6] = 0; first[7] = N - 1
    return pack(b, h, first)
def setup_inputs_lords(rng):
    b, h, first = parts(rng); s = np.arange(N)[:, None, None, None]
    b[:, 0:2] = 7; b[:, 1, int(rng.integers(0, 16))] += rng.integers(0, 2, (N, W))
    b[:, 2:4] = 20 * s + rng.integers(0, 10, (N, 2, 16, W)); b[:, 4] = 255 * rng.integers(0, 2, (N, 1, W))
    b[:, 5] = 255 * (rng.random((N, 16, W)) < rng.random((N, 1, W)))
    m = rng.permutation(TB)[:, None]
    h = np.where(m < TB // 4, h | 255, np.where(m < TB // 2, h | 240, h))
    first[:] = rng.integers(0, N)
    return pack(b, h, first)
def setup_inputs_spread(rng):
    b, h, first = parts(rng)
    b = np.minimum((rng.random((N, 8, 16, W)) * np.exp2(rng.integers(0, 9, (N, 8, 1, W)))).astype(np.int64), 255)
    h = np.minimum((W * rng.random((N, 8, TB, 16)) ** 3).astype(np.int64), W - 1)
    return pack(b, h, np.minimum(first, rng.integers(0, N, (8, TB))))
def check_inputs(d):
    bad = []
    b = np.asarray(d["bk"]).astype(np.float32)
    if not np.all((b >= 0) & (b <= 255) & (b == np.floor(b))): bad.append("numbers of bk")
    for k, hi in (("hand", W - 1), ("ld", N - 1)):
        if np.min(d[k]) < 0 or np.max(d[k]) > hi: bad.append("range of " + k)
    if np.any(d["ld"] != d["ld"][:1]): bad.append("ld alike on all ranks")
    return bad
def reference(bk, hand, ld):
    B = np.asarray(bk).astype(np.float32).astype(np.int16).reshape(N, 8, 16, W)
    c = np.stack([gentries(a) for a in hand]).astype(np.int64).reshape(N, 8, TB, 16)
    lead = np.array(ld[0], np.int64); T = np.zeros(TB, np.int64); won = np.zeros((N, 8, TB), np.int64)
    e = np.zeros((N, 8, TB, 16), np.int64); beat = np.zeros((N, 8, TB, 16), bool); live = np.ones((N, 8, TB, 16), bool)
    S = np.arange(N)[:, None, None]; g = np.arange(8)[:, None]; t = np.arange(TB)[None, :]; R = np.arange(16)
    for deal in range(DE):
        rows, cards, wins = [], [], []
        for k in range(K):
            lr = np.argmax(np.where(live, e, -1), axis=3)[lead, g, t]
            L = c[lead, g, t, lr]; y = B[lead, g, :, L].transpose(0, 2, 1)[..., None]
            isl = S == lead
            live = live & ~(isl[..., None] & (R == lr[..., None]))
            a = ((c * L[..., None] >> 5) + c + 13 * T[:, None]) & (W - 1)
            for s in range(N):
                d = np.take_along_axis(B[s], a[s].reshape(8, 1, -1), 2).reshape(8, 16, TB, 16) - y
                e[s] = np.add.reduce(np.abs(d), axis=1, dtype=np.int64)
                beat[s] = np.add.reduce(d > 0, axis=1, dtype=np.int64) >= 9
            legal = live & ((c & 3) == (L & 3)[..., None])
            legal = np.where(np.any(legal, axis=3, keepdims=True), legal, live)
            good = legal & beat; has = np.any(good, axis=3) & ~isl
            row = np.where(has, np.argmin(np.where(good, e, 2 ** 20), axis=3), np.argmax(np.where(legal, e, -1), axis=3))
            row = np.where(isl, lr, row)[..., None]
            card = np.take_along_axis(c, row, 3)[..., 0]; score = np.where(has, np.take_along_axis(e, row, 3)[..., 0], -1)
            win = np.where(np.any(has, axis=0), np.argmax(score, axis=0), lead)
            live = live & (R != row)
            won = won + (S == win)
            T = np.add.reduce(card[win, g, t] & 255, axis=0)
            lead = win; rows.append(row); cards.append(card); wins.append(win)
        o = np.argsort(np.stack(wins) * K + np.arange(K)[:, None, None], axis=0)
        pile = np.take_along_axis(np.stack(cards), o[:, None], 0).reshape(N, K, 8, TB)
        for k in range(K):
            np.put_along_axis(c, rows[k], pile[:, k][..., None], 3)
            np.put_along_axis(e, rows[k], 0, 3)
        live = np.ones((N, 8, TB, 16), bool)
    return {"yc": np.stack([gtable(a.reshape(8, -1)) for a in c]).astype(np.float32), "yw": won.astype(np.float32)}

from concourse.bass import DstId, RemoteDMATransfer
from concourse.mybir import AluOpType, AxisListType, ActivationFunctionType

ALU = AluOpType
ACT = ActivationFunctionType
NR, W, NT = 4, 4096, 8
MAGIC = 12582912.0
K0 = 2621312.0

POOL = {"f": ("PF", "float32", 8), "h": ("PH", "float16", 16), "b": ("PB", "bfloat16", 16), "i": ("PI", "int32", 8), "u": ("PU", "uint16", 16)}
PIECES = {}
FILL = {"f": 0, "h": 0, "b": 0, "i": 0, "u": 0}


def pieces(text, tail=""):
    for item in text.split():
        name, kind, n = item.split(":")
        al = POOL[kind][2]
        PIECES[name + tail] = (POOL[kind][0], FILL[kind], int(n))
        FILL[kind] += (int(n) + al - 1) // al * al


pieces("rj:f:128 rs:f:128 rg:f:128 r32:f:128 rk:f:128 rv:f:128 rsig:f:128 r4:f:128 rkey:f:32 cols:f:8 cc2:f:16 I32:f:128 seg32:f:8 "
       "tie:f:128 ldf:f:4 m16:f:128 yws:f:256 pi:i:8 J:i:8 t1:i:8 t2:i:8 t3:i:8 li:i:48 I:b:128 Ip128:b:128 Im128:b:128 I12:b:128 "
       "Idead:b:128 Ilead:b:128 Im1:b:128 I4128:b:128 FI:b:256 Seg:b:128 Blk:b:128 Blk2048:b:128 BlkI:b:128 o416:b:128 ones:b:128 "
       "yW:b:256 yK:b:384 wM:b:16 wx:b:24 cW:b:256 cK:b:384 cY:b:128 rs16:b:128 rs4:b:128 Sel:b:640 "
       "lo:u:48 l1:u:8 l2:u:8 l4:u:8 l5:u:8 l7:u:2")
for _h in "01":
    pieces("x:b:2048 M:h:2048 Rm:f:128 Rc:h:128 bt:b:128 Bp:f:128 key:f:128 rm:f:128 oh:b:512 s1:i:8 r:i:16 m2:f:4 m1:f:2 Wn:b:80 "
           "pc:h:512 CD:i:32 m8:i:8 kL:f:128 kL2:f:128 rmL:f:128 fL:f:8 ohl:b:128 lc:h:128 lq:h:128 same:b:128 p:f:128 Z:f:128 yo:u:8 "
           "ys:b:128 Tc:f:1 dg:h:128 z:i:128 a:i:128 ao:u:128 cc:h:128 cq:h:128 cp:h:128 cf:f:128 ci:i:128 c3:i:128 c3f:f:128 "
           "CDf:f:32 kw:f:32 ks:f:32 ka:f:32 cm:f:32 ps:f:32 sel:f:128 pr:f:128 nw:f:128 d:h:512 w32:b:32 w16:b:16 won:b:8", _h)

SCRATCH = {POOL[_k][0]: ("sbuf", [128, FILL[_k]], POOL[_k][1]) for _k in POOL}
SCRATCH.update({
    "win": ("sbuf", [128, W + 16], "bfloat16"), "stB": ("sbuf", [128, 4096], "bfloat16"), "lnB": ("sbuf", [128, 4096], "bfloat16"),
    "stH": ("sbuf", [128, 256], "int32"), "lnH": ("sbuf", [128, 256], "int32"), "hN": ("sbuf", [128, 256], "int32"),
    "ldT": ("sbuf", [128, 4], "int32"), "rx": ("sbuf", [128, 14 * 48], "bfloat16"), "lnW": ("sbuf", [128, 32], "bfloat16"),
    "oc": ("sbuf", [128, 256], "float32"), "lnC": ("sbuf", [128, 256], "float32")})
for _h in "01":
    for _n in "WKMY":
        SCRATCH["b" + _n + _h] = ("psum", [128, 512], "float32")
SEMAPHORES = (["eV", "eS", "eP", "eG", "sent", "aH", "aB0", "aB1", "aB2", "aB3", "aW0", "aW1", "aC0", "aC1"]
              + ["aT%d" % _i for _i in range(14)] + ["d%d" % _i for _i in range(40)])

CV, CP, GATHER, SYNC, SELF, HOP, DMA = 1.0, 0.65, 1.7, 110.0, 60.0, 3800.0, 2200.0
SKEW = [5500.0] * 8
BIAS = {"yoV": 1200.0, "pcP": 2000.0, "rmV": -300.0, "dV": 600.0, "ccP": -1200.0, "rV": 2000.0, "pTP": 3000.0, "cpV": 3000.0, "dgV": 600.0,
        "pP": 3000.0, "aoV": 1200.0, "TcV": -600.0, "RcP": -300.0, "c3fV": -300.0, "pKP": 2000.0, "sV": -300.0, "ccV": 300.0, "pYP": 2000.0}


def order_ops(ops):
    n = len(ops)
    kids = [[] for _ in range(n)]
    for i, o in enumerate(ops):
        for j in o["deps"]:
            kids[j].append(i)

    def gap(j, i):
        a, b = ops[j], ops[i]
        if not b["deps"][j]:
            return 0.0
        return a["lat"] + (SELF if a["eng"] == b["eng"] else SYNC)
    far = [0.0] * n
    for i in range(n - 1, -1, -1):
        far[i] = ops[i]["cost"] + max([gap(i, k) + far[k] for k in kids[i]] + [ops[i]["lat"]])
    left = [len(o["deps"]) for o in ops]
    can = [0.0] * n
    ready, free, seq, end = {}, {}, [], 0.0
    for i in range(n):
        ready.setdefault(ops[i]["eng"], [])
        free.setdefault(ops[i]["eng"], 0.0)
        if left[i] == 0:
            ready[ops[i]["eng"]].append(i)
    while len(seq) < n:
        best = None
        for e, lst in ready.items():
            if lst:
                t0 = max(free[e], min(can[i] for i in lst))
                if best is None or t0 < best[0]:
                    best = (t0, e)
        t0, e = best
        i = max([i for i in ready[e] if can[i] <= t0 + 40.0], key=lambda i: (far[i] + ops[i]["lead"], -i))
        ready[e].remove(i)
        t = max(free[e], can[i]) if e != "A" else can[i]
        fin = t + ops[i]["cost"]
        if e != "A":
            free[e] = fin
        end = max(end, fin + ops[i]["lat"])
        ops[i]["t"] = t
        seq.append(i)
        for k in kids[i]:
            can[k] = max(can[k], fin + gap(i, k))
            left[k] -= 1
            if left[k] == 0:
                ready[ops[k]["eng"]].append(k)
    return seq, end


def emit(g, T, ops, seq):
    q = {"V": g.vector, "S": g.scalar, "P": g.tensor, "G": g, "Y": g.sync}
    need = [False] * len(ops)
    for o in ops:
        for j, sy in o["deps"].items():
            if sy:
                need[j] = True
    count = {"V": 0, "S": 0, "P": 0, "G": 0}
    seen, total, waited = {}, {}, {}
    for i in seq:
        o = ops[i]
        if o["eng"] == "A":
            total[o["sig"][0]] = o["sig"][1]
            continue
        want = {}
        for j, sy in o["deps"].items():
            if sy:
                s, v = ops[j]["sig"]
                want[s] = max(want.get(s, 0), v)
        for s, v in want.items():
            if seen.get((o["eng"], s), 0) < v:
                q[o["eng"]].wait_ge(T.sem[s], v)
                seen[(o["eng"], s)] = v
        ins = o["fn"]()
        if o["kind"] == "dma":
            ins.then_inc(T.sem[o["sig"][0]], 16)
            total[o["sig"][0]] = 16
        elif o["kind"] == "remote":
            total["sent"] = total.get("sent", 0) + o["n"]
        elif need[i]:
            count[o["eng"]] += 1
            o["sig"] = ("e" + o["eng"], count[o["eng"]])
            ins.then_inc(T.sem[o["sig"][0]], 1)
            total[o["sig"][0]] = count[o["eng"]]
    for (e, s), v in seen.items():
        waited[s] = max(waited.get(s, 0), v)
    for s, v in total.items():
        if waited.get(s, 0) < v:
            g.wait_ge(T.sem[s], v)


def build(g, core, T, topo):
    rank = T.rank_of(core)
    peers = [(rank + i) % NR for i in range(1, NR)]
    ops, lastw, readers, lastb, nd, lead = [], {}, {}, {}, [0], [0.0]
    V, S, P = g.vector, g.scalar, g.tensor

    def op(eng, fn, rd=(), wr=(), bank=None, cost=64.0, lat=0.0, kind="op", sig=None, n=0, after=()):
        i = len(ops)
        deps = {}

        def dep(j, data):
            a = ops[j]
            sy = (a["eng"] != eng or (data and eng != "P") or a["kind"] == "dma") and a["kind"] != "remote"
            deps[j] = deps.get(j, False) or sy
        for t in rd:
            if t in lastw:
                dep(lastw[t], True)
        for t in wr:
            if t in lastw:
                dep(lastw[t], True)
            for j in readers.get(t, ()):
                dep(j, True)
        if bank is not None and bank in lastb:
            dep(lastb[bank], False)
        for j in after:
            deps[j] = deps.get(j, False)
        for t in rd:
            readers.setdefault(t, []).append(i)
        for t in wr:
            lastw[t] = i
            readers[t] = []
        if bank is not None:
            lastb[bank] = i
        ops.append({"eng": eng, "fn": fn, "deps": deps, "cost": cost, "lat": lat, "kind": kind, "sig": sig, "n": n, "wr": list(wr), "rd": list(rd),
                    "lead": lead[0] + BIAS.get((list(wr) + list(rd) + ["-"])[0].rstrip("0123456789_") + eng, 0.0)})
        return i

    def A(name, a=0, b=None, step=1, rows=None):
        buf, at, n = PIECES[name]
        b = n if b is None else b
        sl = slice(at + a, at + b, step) if step != 1 else slice(at + a, at + b)
        return T[buf][:, sl] if rows is None else T[buf][0:rows, sl]

    def vcost(n, f=1.0):
        return max(64.0, n * f) * CV

    def ts(out, in0, s1, s2, o0, o1, rd, wr, n, f=1.0, bank=None):
        if o1 is None:
            return op("V", lambda: V.tensor_scalar(out, in0, s1, None, o0), rd, wr, bank, vcost(n, f))
        return op("V", lambda: V.tensor_scalar(out, in0, s1, s2, o0, o1), rd, wr, bank, vcost(n, f))

    def tt(out, in0, in1, o, rd, wr, n, bank=None):
        return op("V", lambda: V.tensor_tensor(out, in0, in1, o), rd, wr, bank, vcost(n, 1.0 if bank else 2.0))

    def tti(out, win, off, in1, o, rd, wr, n):
        return op("V", lambda: V.tensor_tensor(out, win.indirect(off), in1, o), rd, wr, None, 50.0 + GATHER * n * CV)

    def cp(out, in_, rd, wr, n, bank=None):
        return op("V", lambda: V.tensor_copy(out, in_), rd, wr, bank, vcost(n))

    def scan(out, d0, d1, o1, rd, wr, n):
        return op("V", lambda: V.tensor_tensor_scan(out, d0, d1, 0.0, ALU.mult, o1), rd, wr, None, vcost(n))

    def fill(ap, v, rd, wr):
        return op("V", lambda: V.memset(ap, v), rd, wr)

    def mm(bank, out, lhsT, rhs, start, stop, rd, wr, n, f=1.0):
        return op("P", lambda: P.matmul(out, lhsT, rhs, start, stop), rd, wr, bank, max(64.0, n) * f * CP)

    def dma(eng, out, in_, rd, wr, lat=DMA):
        sem = "d%d" % nd[0]
        nd[0] += 1
        qq = g.sync if eng == "Y" else g.scalar
        return op(eng, lambda: qq.dma_start(out, in_), rd, wr, None, 100.0, lat, "dma", (sem, 16))

    def dst(r):
        rid, pid, _ = topo.addr(T.cores[r])
        return DstId(rid=rid, pnc=pid)

    eng_out = [e for e in topo.engines(core, T.cores[peers[0]]) if all(e in topo.engines(core, T.cores[r]) for r in peers)]
    nall = npart = 1
    while nall * 2 <= len(eng_out):
        nall *= 2
    while npart * 2 * len(peers) <= len(eng_out):
        npart *= 2
    mask_all = sum(1 << e for e in eng_out[:nall])

    def send_each(sem, src, dstap, rd, wr):
        trs = [RemoteDMATransfer(dst_ids=[dst(r)], dma_engine_mask=sum(1 << e for e in eng_out[k * npart:(k + 1) * npart]),
                                 remote_sem=T.sem[sem], src=src(r), dst=dstap) for k, r in enumerate(peers)]
        i = op("G", lambda: g.remote_dma_fused(trs, local_sem=T.sem.sent), rd, (), None, 300.0, 0.0, "remote", None, npart * len(peers))
        return op("A", None, (), wr, None, 0.0, HOP, "arr", (sem, npart * len(peers)), 0, [i])

    def send_all(sem, ap, rd, wr):
        tr = RemoteDMATransfer(dst_ids=[dst(r) for r in peers], dma_engine_mask=mask_all, remote_sem=T.sem[sem], srcs=[ap], dsts=[ap] * len(peers))
        i = op("G", lambda: g.remote_dma_fused([tr], local_sem=T.sem.sent), rd, (), None, 300.0, 0.0, "remote", None, nall)
        return op("A", None, (), wr, None, 0.0, HOP, "arr", (sem, nall * len(peers)), 0, [i])

    lead[0] = 9e4
    for k, r in enumerate(peers):
        dma("Y" if k % 2 else "S", T.stH[:, 64 * r:64 * r + 64], T.hand[32 * r:32 * r + 32, :], (), ["stH%d" % r])
    for k, r in enumerate(peers):
        lead[0] = 8e4 - 1e4 * k
        dma("S" if k % 2 else "Y", T.stB[:, 1024 * r:1024 * r + 1024], T.bk[32 * r:32 * r + 32, :], (), ["stB%d" % r], DMA + 600.0 * (k + 1))
    lead[0] = 0.0
    dma("S", T.hN[32 * rank:32 * rank + 32, :], T.hand[32 * rank:32 * rank + 32, :], (), ["hN%d" % rank])
    for h in range(2):
        for b in range(2):
            dma("Y" if b else "S", T.ldT[:, 2 * h + b:2 * h + b + 1], T.ld[2 * rank + b, 128 * h:128 * h + 128], (), ["ld%d%d" % (h, b)])
    dma("S", T.win[32 * rank:32 * rank + 32, 0:W], T.bk[32 * rank:32 * rank + 32, :], (), ["win%d" % rank], DMA + 3000.0)
    send_each("aH", lambda r: T.stH[:, 64 * r:64 * r + 64], T.lnH[:, 64 * rank:64 * rank + 64], ["stH%d" % r for r in peers], ["lnH"])
    prev = len(ops) - 2
    for k, r in enumerate(peers):
        rid, pid, _ = topo.addr(T.cores[r])
        src = (rank - 1 - k) % NR

        def go(r=r, rid=rid, pid=pid):
            return g.remote_dma(T.lnB[:, 1024 * rank:1024 * rank + 1024], T.stB[:, 1024 * r:1024 * r + 1024], T.sem["aB%d" % rank], T.sem.sent, pid, rid, mask_all)
        prev = op("G", go, ["stB%d" % r], (), None, 300.0, 0.0, "remote", None, nall, [prev])
        op("A", None, (), ["lnB%d" % src], None, 0.0, HOP + 3000.0 * (k + 1), "arr", ("aB%d" % src, nall), 0, [prev])
    for k, r in enumerate(peers):
        dma("S" if k % 2 else "Y", T.hN[32 * r:32 * r + 32, :], T.lnH[:, 64 * r:64 * r + 64], ["lnH"], ["hN%d" % r])
    for k in range(NR - 1):
        r = (rank - 1 - k) % NR
        dma("Y", T.win[32 * r:32 * r + 32, 0:W], T.lnB[:, 1024 * r:1024 * r + 1024], ["lnB%d" % r], ["win%d" % r], DMA + 800.0)
    WIN = ["win%d" % r for r in range(NR)] + ["winz"]

    def iota(name, pat, base=0, ch=0, a=0, b=None, tok=None):
        ap, n = A(name, a, b), (PIECES[name][2] if b is None else b - a)
        if PIECES[name][0] == "PF":
            return op("G", lambda: g.iota(ap, pat, base, ch, allow_small_or_imprecise_dtypes=True), (), [name], None, 130.0 + 2 * n)
        return op("G", lambda: g.iota(ap, pat, base, ch), (), [tok or name], None, 130.0 + 2 * n)
    iota("pi", [[0, 8]], 0, 1)
    iota("rj", [[1, 128]])
    iota("rs", [[1, 8], [0, 16]])
    iota("rg", [[0, 4], [1, 2], [0, 16]])
    iota("r32", [[0, 4], [1, 32]])
    iota("rk", [[0, 8], [1, 16]])
    iota("rv", [[16, 4], [0, 2], [-1, 16]], 15)
    iota("rsig", [[1, 4], [0, 32]])
    iota("r4", [[0, 32], [1, 4]])
    iota("rkey", [[0, 2], [1, 4], [4, 4]])
    iota("J", [[16, 8]])
    iota("li", [[16, 8]], 15, 0, 0, 8, "li0")
    iota("li", [[1, 8]], 0, 0, 8, 16, "li1")
    iota("li", [[4, 4], [16, 8]], 3, 0, 16, 48, "li2")
    cp(A("lo"), A("li"), ["li0", "li1", "li2"], ["lo"], 48)
    sh, an, mul, add = ALU.arith_shift_right, ALU.bitwise_and, ALU.mult, ALU.add
    ts(A("pi", 1, 2), A("pi", 0, 1), 4, None, sh, None, ["pi"], ["pi1"], 1)
    ts(A("pi", 2, 3), A("pi", 0, 1), 4, 1, sh, an, ["pi"], ["pi2"], 1)
    ts(A("pi", 3, 4), A("pi", 0, 1), 31, None, an, None, ["pi"], ["pi3"], 1)
    ts(A("pi", 4, 5), A("pi", 0, 1), 15, None, an, None, ["pi"], ["pi4"], 1)
    ts(A("pi", 5, 6), A("pi", 0, 1), 4.0, 3.0, mul, add, ["pi"], ["pi5"], 1)
    cp(A("cols"), A("pi"), ["pi", "pi1", "pi2", "pi3", "pi4", "pi5"], ["cols"], 8)

    def eqm(name, a, row, step, col, w):
        ts(A(name, a, a + 128 // step), A(row, 0, 128, step), A("cols", col, col + 1), float(w), ALU.is_equal, mul, [row, "cols"], [name + str(a)], 128 // step)
        return name + str(a)
    for nm, w in [("I", 1), ("I32", 1), ("Ip128", 128), ("Im128", -128), ("I12", 2.0 ** -12), ("Idead", -2.0 ** 22), ("Ilead", 2.0 ** 22), ("Im1", -1), ("I4128", 4128)]:
        eqm(nm, 0, "rj", 1, 0, w)
    FI = [eqm("FI", a, "rj", 1, 0, 2.0 ** 19) for a in (0, 128)]
    eqm("Seg", 0, "rs", 1, 1, 1)
    eqm("Blk", 0, "rg", 1, 2, 1)
    eqm("Blk2048", 0, "rg", 1, 2, 2048)
    eqm("BlkI", 0, "r32", 1, 3, 1)
    eqm("m16", 0, "rk", 1, 4, 1)
    eqm("seg32", 0, "rs", 16, 1, 1)
    for c in range(5):
        ts(A("Sel", 128 * c, 128 * c + 128), A("rj"), 128.0 * c, A("cols", 5, 6), add, ALU.is_equal, ["rj", "cols", "Sel0"], ["Sel0"], 128)
    yW = [eqm("yW", a, "rg", 1, 2, -1) for a in (0, 128)]
    yK = [eqm("yK", a, "rg", 1, 2, w) for a, w in ((0, 64), (128, -64), (256, 2.0 ** -13))]
    wM = [eqm("wM", a, "rs", 16, 1, 1) for a in (0, 8)]
    wx = [eqm("wx", a, "rs", 16, 1, w) for a, w in ((0, -64), (8, 64), (16, -2.0 ** -13))]
    fill(A("o416"), 416.0, (), ["o416"])
    fill(A("ones"), 1.0, (), ["ones"])
    fill(T.win[:, W:W + 16], 0.0, (), ["winz"])
    fill(T.rx[:, 32:14 * 48:48], -2048.0, (), ["rxc"])
    ts(A("rs16"), A("rk"), 0.0, None, ALU.not_equal, None, ["rk"], ["rs16"], 128)
    ts(A("rs4"), A("r4"), 0.0, None, ALU.not_equal, None, ["r4"], ["rs4"], 128)
    ts(A("tie"), A("rk"), -2.0 ** -17, 2.0 ** -13, mul, add, ["rk"], ["tie"], 128)
    e0, e1, e2 = A("I32", 0, 1), A("I32", 1, 2), A("I32", 2, 3)

    def c2(c):
        return A("cc2", c, c + 1)
    for c, (col, w) in enumerate([(e0, 9 * 2.0 ** 17), (e0, 11 * 2.0 ** 17), (e0, 0.25), (e0, 2048.0), (e0, -128.0), (e0, -15.0 / 32), (e1, -64.0),
                                  (e1, -0.5), (e1, 1.0 / 16), (e2, -2.0 ** -10)]):
        ts(c2(c), col, w, None, mul, None, ["I320"], ["cc%d" % c], 1)
    tt(c2(10), c2(1), c2(6), add, ["cc1", "cc6"], ["cc10"], 1)
    tt(c2(11), c2(3), c2(7), add, ["cc3", "cc7"], ["cc11"], 1)
    ts(A("cK", 0, 128), A("rv"), e1, c2(0), mul, add, ["rv", "I320", "cc0"], ["cK0"], 128)
    ts(A("cK", 128, 256), A("rv"), e1, c2(10), mul, add, ["rv", "I320", "cc10"], ["cK1"], 128)
    ts(A("cK", 256, 384), A("tie"), e1, c2(2), mul, add, ["tie", "I320", "cc2"], ["cK2"], 128)
    ts(A("cW", 0, 128), A("ones"), c2(9), c2(11), mul, add, ["ones", "cc9", "cc11"], ["cW0"], 128)
    ts(A("cW", 128, 256), A("ones"), c2(5), None, mul, None, ["ones", "cc5"], ["cW1"], 128)
    ts(A("cY"), A("ones"), c2(4), c2(8), mul, add, ["ones", "cc4", "cc8"], ["cY"], 128)
    ts(A("J"), A("J"), A("cols", 4, 5), None, add, None, ["J", "cols"], ["J"], 8)

    def lst(name, terms, plus):
        for nm, (s_, m_, w_) in zip(("t1", "t2", "t3"), terms):
            ts(A(nm), A("J"), s_, m_, sh, an, ["J", nm], [nm], 8)
            ts(A(nm), A(nm), float(w_), None, mul, None, [nm], [nm], 8)
        for nm in ("t2", "t3")[:len(terms) - 1]:
            tt(A("t1"), A("t1"), A(nm), add, ["t1", nm], ["t1"], 8)
        ts(A(name), A("t1"), float(plus), None, add, None, ["t1"], [name], 8)
    lst("l1", [(4, 1, 1), (2, 3, 8), (0, 3, 2)], 0)
    lst("l2", [(2, 7, 4)], 3)
    lst("l4", [(4, 1, 16), (0, 3, 4)], 3)
    lst("l5", [(4, 1, 1), (2, 3, 2), (0, 3, 8)], 0)
    ts(A("t1", 0, 2), A("pi", 6, 8), 1, None, an, None, ["pi"], ["t1"], 2)
    cp(A("l7"), A("t1", 0, 2), ["t1"], ["l7"], 2)

    def cards(h, ci, CI):
        cp(A("cc" + h), A("cf" + h), ["cf" + h], ["cc" + h], 128)
        ts(A("c3" + h), ci, 3, None, an, None, CI, ["c3" + h], 128)
        cp(A("c3f" + h), A("c3" + h), ["c3" + h], ["c3f" + h], 128)
        ts(A("cq" + h), A("c3f" + h), -2048.0, None, add, None, ["c3f" + h], ["cq" + h], 128)
        tt(A("cp" + h), A("cf" + h), A("c3f" + h), ALU.subtract, ["cf" + h, "c3f" + h], ["cp" + h], 128)

    HN = ["hN%d" % r for r in range(NR)]
    cp(A("ldf"), T.ldT[:, 0:4], ["ld00", "ld01", "ld10", "ld11"], ["ldf"], 4)
    for hh in range(2):
        h = str(hh)
        hn = T.hN[:, 128 * hh:128 * hh + 128]
        ts(A("cf" + h), hn, -2048.0, None, add, None, HN, ["cf" + h], 128)
        cards(h, hn, HN)
        fill(A("ohl" + h), 0.0, (), ["ohl" + h])
        fill(A("r" + h, 8, 16), 0, (), ["rpad" + h])
        fill(A("Tc" + h), -2048.0, (), ["Tc" + h])
        for b in range(2):
            ts(A("ohl" + h, 16 * b, 128, 32), A("r4", 0, 4), A("ldf", 2 * hh + b, 2 * hh + b + 1), None, ALU.is_equal, None,
               ["r4", "ldf", "ohl" + h], ["ohl" + h], 4)

    def trick(n, hh):
        h, j = str(hh), n % 4
        bW, bK, bM, bY = T["bW" + h], T["bK" + h], T["bM" + h], T["bY" + h]
        kW, kK, kM, kY = "W" + h, "K" + h, "M" + h, "Y" + h

        def B(name, a=0, b=None, step=1):
            return A(name + h, a, b, step)

        def N(*names):
            return [x + h for x in names]
        mm(kM, bM[:, 0:128], B("ohl"), A("I"), True, True, N("ohl") + ["I0"], N("pO"), 128)
        tt(B("lc"), bM[:, 0:128], B("cp"), mul, N("pO", "cp"), N("lc"), 128, kM)
        tt(B("lq"), bM[:, 0:128], B("cq"), mul, N("pO", "cq"), N("lq"), 128, kM)
        mm(kM, bM[:, 384:512], B("lc"), A("Seg"), True, False, N("lc") + ["Seg0"], (), 128)
        mm(kM, bM[:, 384:512], B("lq"), A("Seg"), False, True, N("lq"), N("pZ"), 128)
        mm(kM, bM[:, 128:256], A("Blk"), B("lc"), True, False, N("lc") + ["Blk0"], (), 128)
        mm(kM, bM[:, 128:256], A("Blk"), B("lq"), False, True, N("lq"), N("pL"), 128)
        mm(kM, bM[:, 256:384], A("Blk"), B("lq"), True, True, N("lq"), N("p3"), 128)
        mm(kW, bW[:, 0:128], A("I4128"), B("cc"), True, False, N("cc") + ["I41280"], (), 128)
        mm(kW, bW[:, 0:128], A("Blk2048"), B("lc"), False, False, N("lc") + ["Blk20480"], (), 128)
        mm(kW, bW[:, 0:128], A("Blk2048"), B("lq"), False, False, N("lq"), (), 128)
        tt(B("Z"), bM[:, 384:512], A("m16"), mul, N("pZ") + ["m160"], N("Z"), 128, kM)
        mm(kY, bY[:, 128:136], B("Z"), A("seg32"), True, True, N("Z") + ["seg320"], N("pY"), 64, 4.0)
        ts(B("yo"), bY[:, 128:136], float(W), None, add, None, N("pY"), N("yo"), 8, 1.0, kY)
        op("S", lambda: S.activation(B("ys"), T.win[:, 0:W + 16].indirect(B("yo")), ACT.Copy), N("yo") + WIN, N("ys"), None, 65.0 + GATHER * 128 * CV)
        mm(kY, bY[:, 0:128], A("ones", rows=4), A("cY", rows=4), True, False, ["ones", "cY"], (), 128)
        mm(kY, bY[:, 0:128], A("BlkI"), B("ys"), False, True, N("ys") + ["BlkI0"], N("py"), 128)
        tt(B("p"), bM[:, 128:256], B("cc"), mul, N("pL", "cc"), N("p"), 128, kM)
        tt(B("same"), bM[:, 256:384], B("cq"), ALU.is_equal, N("p3", "cq"), N("same"), 128, kM)
        if n > 0:
            at0 = 48 * (2 * (n - 1) + hh)
            op("V", lambda: V.tensor_reduce(B("Tc"), T.rx[:, at0:at0 + 33], AxisListType.X, add), ["rxc", "rx%d" % at0, "own%d" % at0], N("Tc"))
        ts(B("dg"), A("I"), B("Tc"), None, mul, None, N("Tc") + ["I0"], N("dg"), 128, 0.5)
        mm(kW, bW[:, 0:128], A("o416"), B("dg"), False, True, N("dg") + ["o416"], N("pT"), 128)
        tt(B("z"), bW[:, 0:128], B("p"), add, N("pT", "p"), N("z"), 128, kW)
        ts(B("a"), B("z"), 5, W - 1, sh, an, N("z"), N("a"), 128)
        cp(B("ao"), B("a"), N("a"), N("ao"), 128)
        for c in range(4):
            op("S", lambda c=c: S.activation(B("x", 512 * c, 512 * c + 512), T.win[:, 0:W + 16].indirect(B("ao", 32 * c, 32 * c + 32)), ACT.Identity, bias=-128.0),
               N("ao") + WIN, N("x%d_" % c), None, 65.0 + GATHER * 512 * CV)
        X = N("x0_", "x1_", "x2_", "x3_")
        mm(kW, bW[:, 0:256], A("ones", rows=4), A("cW", rows=4), True, False, ["ones", "cW0", "cW1"], (), 256)
        mm(kW, bW[:, 0:256], B("ys"), A("yW"), False, False, N("ys") + yW, (), 256)
        mm(kK, bK[:, 0:384], A("ones", rows=4), A("cK", rows=4), True, False, ["ones", "cK0", "cK1", "cK2"], (), 384)
        mm(kK, bK[:, 0:384], B("ys"), A("yK"), False, False, N("ys") + yK, (), 384)
        mm(kK, bK[:, 0:256], B("same"), A("FI"), False, False, N("same") + FI, (), 256)
        mm(kK, bK[:, 0:128], A("Ilead"), B("ohl"), False, False, N("ohl") + ["Ilead0"], (), 128)
        for i in range(j):
            for a, nm in ((0, "Idead"), (128, "Idead"), (256, "Im1")):
                mm(kK, bK[:, a:a + 128], A(nm), B("oh", 128 * i, 128 * i + 128), False, False, N("oh%d_" % i) + [nm + "0"], (), 128)
        for k in range(16):
            mm(kK, bK[:, k:384:16], B("x", k, 2048, 16), A("wx"), False, False, X + wx, (), 24)
        for c in range(2):
            for k in range(16):
                tt(B("M", 128 * k + 64 * c, 128 * k + 64 * c + 64), B("x", 1024 * c + k, 1024 * c + 1024, 16), bY[:, 64 * c:64 * c + 64], ALU.max,
                   X[2 * c:2 * c + 2] + N("py"), N("M%d_%d_" % (k, c)), 64, kY)
        for k in range(16):
            mm(kW, bW[:, k:256:16], B("M", 128 * k, 128 * k + 128), A("wM"), False, k == 15, N("M%d_0_" % k, "M%d_1_" % k) + wM, N("pW") if k == 15 else (), 16)
        op("S", lambda: S.activation(B("Rm"), bW[:, 0:128], ACT.Identity, bias=MAGIC, scale=1.0 + 2.0 ** -13), N("pW"), N("Rm"), kW, vcost(128))
        ts(B("Rc"), B("Rm"), -(MAGIC + 2048.0), None, add, None, N("Rm"), N("Rc"), 128)
        mm(kK, bK[:, 128:256], A("Im128"), B("Rc"), False, False, N("Rc") + ["Im1280"], (), 128)
        mm(kK, bK[:, 0:128], A("Ip128"), B("Rc"), False, False, N("Rc") + ["Ip1280"], (), 128)
        mm(kK, bK[:, 256:384], A("I12"), B("Rc"), False, True, N("Rc") + ["I120"], N("pK"), 128)
        tt(B("bt"), bW[:, 128:256], B("Rc"), ALU.is_le, N("pW", "Rc"), N("bt"), 128, kW)
        tt(B("Bp"), bK[:, 128:256], B("bt"), mul, N("pK", "bt"), N("Bp"), 128, kK)
        tt(B("key"), bK[:, 0:128], B("Bp"), ALU.max, N("pK", "Bp"), N("key"), 128, kK)
        scan(B("rm"), A("rs16"), B("key"), ALU.max, N("key") + ["rs16"], N("rm"), 128)
        oh, OH = B("oh", 128 * j, 128 * j + 128), N("oh%d_" % j)
        tti(oh, B("rm"), A("lo", 0, 8), B("key"), ALU.is_equal, N("rm", "key") + ["lo"], OH, 128)
        ts(B("s1"), B("rm", 15, 128, 16), K0, 2.0 ** 18, ALU.min, add, N("rm"), N("s1"), 8)
        ts(B("r", 0, 8), B("s1"), 4, 32767, sh, an, N("s1"), N("r"), 8)
        tt(B("m2"), B("r", 0, 4), B("r", 4, 8), ALU.min, N("r"), N("m2"), 4)
        tt(B("m1"), B("m2", 0, 2), B("m2", 2, 4), ALU.min, N("m2"), N("m1"), 2)
        WN, wn = N("Wn%d_" % n), B("Wn", 8 * n, 8 * n + 8)
        tti(B("Wn", 8 * n, 8 * n + 16), B("m1"), A("l7", 0, 1), B("r"), ALU.is_equal, N("r", "m1", "rpad") + ["l7"], WN + N("Wn%d_" % (n + 1)), 16)
        mm(kW, bW[:, 256:384], oh, A("I"), True, True, OH + ["I0"], N("pP"), 128)
        pc, PC = B("pc", 128 * j, 128 * j + 128), N("pc%d_" % j)
        tt(pc, bW[:, 256:384], B("cc"), mul, N("pP", "cc"), PC, 128, kW)
        mm(kW, bW[:, 384:392], pc, A("wM", 0, 8), True, True, PC + wM, N("pC"), 8)
        cp(B("CD", 8 * j, 8 * j + 8), bW[:, 384:392], N("pC"), N("CD%d_" % j), 8, kW)
        if n < NT - 1:
            at = 48 * (2 * n + hh)
            mine = T.rx[:, at + 8 * rank:at + 8 * rank + 8]
            ts(B("m8"), B("CD", 8 * j, 8 * j + 8), 255, None, an, None, N("CD%d_" % j), N("m8"), 8)
            tt(mine, B("m8"), wn, mul, N("m8") + WN, ["own%d" % at], 8)
            send_all("aT%d" % (2 * n + hh), mine, ["own%d" % at], ["rx%d" % at])
            tt(B("kL"), bK[:, 256:384], oh, ALU.subtract, N("pK") + OH, N("kL"), 128, kK)
            kl = "kL"
            if j == 3:
                tt(B("kL2"), B("kL"), A("tie"), ALU.max, N("kL") + ["tie"], N("kL2"), 128)
                kl = "kL2"
            scan(B("rmL"), A("rs16"), B(kl), ALU.max, N(kl) + ["rs16"], N("rmL"), 128)
            tt(B("fL"), B("rmL", 15, 128, 16), wn, mul, N("rmL") + WN, N("fL"), 8)
            tti(B("ohl"), B("fL"), A("lo", 8, 16), B(kl), ALU.is_equal, N("fL", kl) + ["lo"], N("ohl"), 128)
        else:
            tt(B("w32"), B("Wn", 0, 32), B("Wn", 32, 64), add, N(*["Wn%d_" % i for i in range(NT)]), N("w32"), 32)
            tt(B("w16"), B("w32", 0, 16), B("w32", 16, 32), add, N("w32"), N("w16"), 16)
            tt(B("won"), B("w16", 0, 8), B("w16", 8, 16), add, N("w16"), N("won"), 8)
            lw = T.lnW[:, 16 * hh + 2 * rank:16 * hh + 2 * rank + 2]
            send_each("aW" + h, lambda r: B("won", 2 * r, 2 * r + 2), lw, N("won"), N("lnW"))
            cp(lw, B("won", 2 * rank, 2 * rank + 2), N("won", "lnW"), N("lnW2"), 2)
            mm(kM, bM[0:8, 0:128], T.lnW[:, 16 * hh:16 * hh + 8], A("I"), True, True, N("lnW", "lnW2"), N("pO"), 128)
            ywp = A("yws", 128 * hh, 128 * hh + 128, 1, 8)
            cp(ywp, bM[0:8, 0:128], N("pO"), N("yws"), 128, kM)
            dma("S", T.yw[:, 128 * hh:128 * hh + 128], ywp, N("yws"), ())
        if j < 3:
            return
        WD = N(*["Wn%d_" % i for i in range(n - 3, n + 1)])
        cp(B("CDf"), B("CD"), N("CD0_", "CD1_", "CD2_", "CD3_"), N("CDf"), 32)
        tti(B("kw"), B("Wn", 8 * (n - 3), 8 * (n + 1)), A("l1", 0, 2), A("rkey"), mul, WD + ["l1", "rkey"], N("kw"), 32)
        scan(B("ks"), A("rs4", 0, 32), B("kw"), add, N("kw") + ["rs4"], N("ks"), 32)
        op("V", lambda: V.tensor_copy(B("ka"), B("ks").indirect(A("l2", 0, 2))), N("ks") + ["l2"], N("ka"), None, 100.0)
        tti(B("cm"), B("ks"), A("l4", 0, 2), B("ka"), ALU.is_lt, N("ks", "ka") + ["l4"], N("cm"), 32)
        scan(B("ps"), A("rs4", 0, 32), B("cm"), add, N("cm"), N("ps"), 32)
        tti(B("sel"), B("ps"), A("l4"), A("rsig"), ALU.is_equal, N("ps") + ["rsig"], N("sel"), 128)
        tti(B("pr"), B("CDf"), A("l5"), B("sel"), mul, N("CDf", "sel") + ["l5"], N("pr"), 128)
        scan(B("nw"), A("rs4"), B("pr"), add, N("pr"), N("nw"), 128)
        mm(kY, bY[:, 256:384], A("I"), B("cc"), True, False, N("cc"), (), 128)
        for i in range(4):
            mm(kY, bY[:, 256:384], A("Im1"), B("pc", 128 * i, 128 * i + 128), False, False, N("pc%d_" % i), (), 128)
        for i in range(4):
            d = B("d", 128 * i, 128 * i + 128)
            tti(d, B("nw"), A("lo", 16 + 8 * i, 24 + 8 * i), B("oh", 128 * i, 128 * i + 128), mul, N("nw", "oh%d_" % i), N("d%d_" % i), 128)
            mm(kY, bY[:, 256:384], d, A("I"), False, i == 3, N("d%d_" % i), N("pD") if i == 3 else (), 128)
        if n < NT - 1:
            cp(B("ci"), bY[:, 256:384], N("pD"), N("ci"), 128, kY)
            op("S", lambda: S.activation(B("cf"), bY[:, 256:384], ACT.Copy), N("pD"), N("cf"), kY, 128.0)
            cards(h, B("ci"), N("ci"))
            return
        cp(B("cp"), bY[:, 256:384], N("pD"), N("cp"), 128, kY)
        for s in range(NR):
            for qq in range(4):
                mm(kK, bK[:, 32 * s:32 * s + 32], A("Sel", 128 * s - qq + 3, 128 * s - qq + 131), B("cp", 32 * qq, 32 * qq + 32), qq == 0, qq == 3,
                   N("cp") + ["Sel0"], N("pK") if s == 3 and qq == 3 else (), 32)
        o0 = 128 * hh
        ts(T.oc[:, o0:o0 + 128], bK[:, 0:128], 2048.0, None, add, None, N("pK"), N("oc"), 128, 1.0, kK)
        send_each("aC" + h, lambda r: T.oc[:, o0 + 32 * r:o0 + 32 * r + 32], T.lnC[:, o0 + 32 * rank:o0 + 32 * rank + 32], N("oc"), N("lnC"))
        dma("Y", T.yc[32 * rank:32 * rank + 32, o0:o0 + 128], T.oc[:, o0 + 32 * rank:o0 + 32 * rank + 32], N("oc"), ())
        for k, r in enumerate(peers):
            dma("S" if k % 2 else "Y", T.yc[32 * r:32 * r + 32, o0:o0 + 128], T.lnC[:, o0 + 32 * r:o0 + 32 * r + 32], N("lnC"), ())

    for n in range(NT):
        for hh in range(2):
            lead[0] = SKEW[n] if hh == 0 else 0.0
            trick(n, hh)
    return ops


def rank_program(g, core, T, topo):
    if T.rank_of(core) is None:
        return
    ops = build(g, core, T, topo)
    seq, _ = order_ops(ops)
    emit(g, T, ops, seq)
